import numpy as np
import ml_dtypes


def mxq(x, axis, fmt="e4m3"):
    dtype, down = {"e4m3": (ml_dtypes.float8_e4m3fn, 7), "e5m2": (ml_dtypes.float8_e5m2, 14)}[fmt]
    v = np.moveaxis(np.asarray(x, np.float32).astype(ml_dtypes.bfloat16).astype(np.float64), axis, -1)
    blocks = v.reshape(v.shape[:-1] + (-1, 32))
    amax = np.abs(blocks).max(-1, keepdims=True)
    byte = np.maximum(np.where(amax > 0, np.frexp(amax)[1] - 1 + 127, 0) - down, 1)
    scale = np.exp2(byte - 127.0)
    codes = (blocks / scale).astype(np.float32).astype(dtype).astype(np.float64)
    return np.moveaxis((codes * scale).reshape(v.shape), -1, axis)


WIDE = False


def mx_kscale(k):
    if not WIDE:
        return np.ones(k)
    levels = np.array([10, -10, 5, -5, 0])
    if k % 512:
        return np.exp2(np.random.permutation(np.resize(levels, k // 32))).repeat(32)
    a = np.empty((k // 512, 16))
    for p in range(k // 512):
        a[p, :8] = np.random.permutation(np.resize(levels, 8))
        for g in range(8):
            far = levels[np.abs(levels - a[p, g]) >= 10]
            a[p, g + 8] = far[np.random.randint(len(far))]
    return np.exp2(a.ravel()).repeat(32)


def f64(x):
    return np.asarray(x).astype(np.float64)


def striped(idx):
    return np.tile(idx.reshape(-1, 16).T, (8, 1)).astype(np.uint16)


def unstriped(offs):
    return offs[:16].T.reshape(-1).astype(np.int64)


def pack_weight(w):
    k, n = w.shape
    w = f64(np.asarray(w, np.float32).astype(ml_dtypes.bfloat16)).reshape(k // 32, 32, n)
    amax = np.abs(w).max(1)
    byte = np.clip(np.where(amax > 0, np.frexp(amax)[1] - 1 + 127 - 7, 1), 1, 254)
    scaled = (w * np.exp2(127.0 - byte)[:, None, :]).reshape(k, n).astype(np.float32)
    words = np.ascontiguousarray(scaled.reshape(k // 512, 128, 4, n).transpose(0, 1, 3, 2)).astype(ml_dtypes.float8_e4m3fn).view(np.uint8)
    return words, np.ascontiguousarray(byte.astype(np.uint8).reshape(k // 512, 16, n))


def unpack_weight(words, scales):
    g, p, n, _ = words.shape
    vals = np.ascontiguousarray(words).view(ml_dtypes.float8_e4m3fn).astype(np.float64) * np.repeat(np.exp2(scales.astype(np.float64) - 127.0), 8, axis=1)[..., None]
    return vals.transpose(0, 1, 3, 2).reshape(g * 512, n)


K, T, E, C, N = 512, 4096, 16, 128, 128


def by_expert(wq, xq):
    return np.concatenate([wq[e].T @ xq[:, e * C:(e + 1) * C] for e in range(E)], axis=1)


def setup_inputs():
    n = np.random.standard_normal
    s = mx_kscale(K)[:, None]
    packed = [pack_weight(m) for m in n((E, K, N)) / np.sqrt(K) / s[None]]
    return {
        "xT": (n((K, T)) * s).astype(np.float32),
        "w_words": np.stack([m[0] for m in packed]),
        "w_scales": np.stack([m[1] for m in packed]),
        "b": (0.3 * n((N, E))).astype(np.float32),
        "gate": np.tile(np.random.uniform(0.2, 1.0, E * C), (N, 1)).astype(np.float32),
        "offs": striped(np.random.permutation(T)[:E * C]),
    }


def reference(xT, w_words, w_scales, b, gate, offs):
    idx = unstriped(offs)
    xq = mxq(f64(xT)[:, idx], 0, "e4m3")
    w = np.stack([unpack_weight(w_words[e], w_scales[e]) for e in range(E)])
    y = by_expert(w, xq)
    y = y + np.repeat(f64(b), C, axis=1)
    out = np.zeros((N, T))
    out[:, idx] = f64(gate) * y
    return out

@@ -1,0 +1,120 @@
+from contextlib import ExitStack
+
+import concourse.mybir as mybir
+
+F32 = mybir.dt.float32
+BF16 = mybir.dt.bfloat16
+I32 = mybir.dt.int32
+U32 = mybir.dt.uint32
+U16 = mybir.dt.uint16
+U8 = mybir.dt.uint8
+FP8X4 = mybir.dt.float8_e4m3fn_x4
+
+P = 128
+K, T, E, C, N = 512, 4096, 16, 128, 128
+SLOTS = E * C
+FLOPS = 2 * K * N * SLOTS
+
+IDX_COL = 16
+GATHER = 1024
+SLICE = 512
+PIECES = (
+    ((1024, 256), (1024, 256), (1024, 256), (1024, 384)),
+    ((1024, 256), (1024, 256), (1024, 384), (512, 320), (512, 320)),
+)
+
+
+def tile_routed_moe_kernel(tc, xT, w_words, w_scales, b, gate, offs, out):
+    nc = tc.nc
+    with ExitStack() as ctx:
+        held = ctx.enter_context(tc.tile_pool(name="held", bufs=1))
+        psum = ctx.enter_context(tc.psum_pool(name="psum", bufs=1))
+
+        offsets = held.tile([P, SLOTS // IDX_COL], U16, name="offsets")
+        x_view = xT.rearrange("(p u r) n -> u p r n", u=2, r=2)
+        raws = []
+        for u in range(2):
+            start = 0
+            for i, (width, v_width) in enumerate(PIECES[u]):
+                raw = held.tile([P, 2, width], F32, name=f"raw_{u}_{i}")
+                nc.sync.dma_start(raw[:], x_view[u][:, :, start : start + width])
+                raws.append((u, start, width, v_width, raw))
+                start += width
+            if u == 0:
+                nc.sync.dma_start(offsets[:], offs)
+
+        bias = held.tile([P, E], F32, name="bias")
+        w_sc = held.tile([P, E * N], U8, name="w_sc", align_bytes=64)
+        nc.vector.memset(w_sc[:].bitcast(I32), 0)
+        window = held.tile([P, T], F32, name="window")
+        nc.vector.memset(window[:], 0.0)
+
+        sc_view = w_scales.rearrange("e a q n -> q (e a) n").bitcast(I32)
+        w_sc_view = w_sc[:].rearrange("p (e n) -> p e n", e=E).bitcast(I32)
+        for q in range(4):
+            nc.sync.dma_start(w_sc_view[32 * q : 32 * q + 4], sc_view[4 * q : 4 * q + 4])
+        nc.sync.dma_start(bias[:], b)
+        w_codes = held.tile([P, E * N], U32, name="w_codes", align_bytes=64)
+        words_view = w_words.rearrange("e a p n r -> p (e a) (n r)").bitcast(I32)
+        w_codes_view = w_codes[:].rearrange("p (e n) -> p e n", e=E).bitcast(I32)
+        for h in range(2):
+            es = slice(h * E // 2, (h + 1) * E // 2)
+            nc.sync.dma_start(w_codes_view[:, es, :], words_view[:, es, :])
+        gates = []
+        for h in range(2):
+            g = held.tile([P, SLOTS // 2], F32, name=f"gate_{h}")
+            nc.sync.dma_start(g[:], gate[:, h * (SLOTS // 2) : (h + 1) * (SLOTS // 2)])
+            gates.append(g)
+
+        pairs = [held.tile([P, 2 * T], BF16, name=f"pair_{u}") for u in range(2)]
+        grouped = [held.tile([P, 4 * GATHER], BF16, name=f"grouped_{g}", align_bytes=64) for g in range(SLOTS // GATHER)]
+        for u in range(2):
+            pair = pairs[u][:].rearrange("p (n r) -> p n r", r=2)
+            for (uu, start, width, v_width, raw) in raws:
+                if uu != u:
+                    continue
+                src = raw[:].rearrange("p r n -> p n r")
+                nc.vector.tensor_copy(pair[:, start : start + v_width, :], src[:, :v_width, :])
+                nc.scalar.copy(pair[:, start + v_width : start + width, :], src[:, v_width:, :])
+            for g in range(SLOTS // GATHER):
+                idx = offsets[:, g * GATHER // IDX_COL : (g + 1) * GATHER // IDX_COL]
+                dst = grouped[g][:].bitcast(U32).rearrange("p (n u) -> p n u", u=2)[:, :, u]
+                nc.vector.tensor_copy(dst, pairs[u][:].bitcast(U32).indirect(idx))
+
+        for s in range(SLOTS // SLICE):
+            codes = held.tile([P, SLICE], U32, name=f"codes_{s}", align_bytes=64)
+            scales = held.tile([P, SLICE], U8, name=f"scales_{s}", align_bytes=64)
+            g, off = divmod(s * SLICE, GATHER)
+            nc.vector.quantize_mx(
+                out=codes[:].bitcast(FP8X4), scales=scales[:], in_=grouped[g][:, 4 * off : 4 * (off + SLICE)]
+            )
+            acc = psum.tile([P, SLICE], F32, name=f"acc_{s}")
+            sums = held.tile([P, SLICE], F32, name=f"sums_{s}")
+            for i in range(SLICE // C):
+                e = s * (SLICE // C) + i
+                cols = slice(i * C, (i + 1) * C)
+                w_cols = slice(e * N, (e + 1) * N)
+                nc.tensor.matmul_mx(
+                    out=acc[:, cols],
+                    lhsT=w_codes[:, w_cols].bitcast(FP8X4),
+                    lhsT_scale=w_sc[:, w_cols],
+                    rhs=codes[:, cols].bitcast(FP8X4),
+                    rhs_scale=scales[:, cols],
+                    start=True,
+                    stop=True,
+                )
+            for i in range(SLICE // C):
+                e = s * (SLICE // C) + i
+                cols = slice(i * C, (i + 1) * C)
+                nc.scalar.activation(
+                    sums[:, cols], acc[:, cols], mybir.ActivationFunctionType.Identity, bias=bias[:, e : e + 1]
+                )
+            h, off = divmod(s * SLICE, SLOTS // 2)
+            nc.vector.tensor_tensor(
+                window[:].indirect(offsets[:, s * SLICE // IDX_COL : (s + 1) * SLICE // IDX_COL]),
+                sums[:],
+                gates[h][:, off : off + SLICE],
+                mybir.AluOpType.mult,
+            )
+        nc.sync.dma_start(out[:, : T // 2], window[:, : T // 2])
+        nc.scalar.dma_start(out[:, T // 2 :], window[:, T // 2 :])

@@ -16,12 +16,12 @@ SLOTS = E * C
 FLOPS = 2 * K * N * SLOTS
 
 IDX_COL = 16
-GATHER = 1024
 SLICE = 512
 PIECES = (
-    ((1024, 256), (1024, 256), (1024, 256), (1024, 384)),
-    ((1024, 256), (1024, 256), (1024, 384), (512, 320), (512, 320)),
+    ((1024, 512), (1024, 512), (1024, 512), (1024, 512)),
+    ((1024, 512), (1024, 512), (1024, 512), (512, 320), (512, 320)),
 )
+GATHERS = ((1024, 1024), (512, 512, 512, 512))
 
 
 def tile_routed_moe_kernel(tc, xT, w_words, w_scales, b, gate, offs, out):
@@ -67,7 +67,7 @@ def tile_routed_moe_kernel(tc, xT, w_words, w_scales, b, gate, offs, out):
             gates.append(g)
 
         pairs = [held.tile([P, 2 * T], BF16, name=f"pair_{u}") for u in range(2)]
-        grouped = [held.tile([P, 4 * GATHER], BF16, name=f"grouped_{g}", align_bytes=64) for g in range(SLOTS // GATHER)]
+        gathered = held.tile([P, 2, SLOTS], U32, name="gathered")
         for u in range(2):
             pair = pairs[u][:].rearrange("p (n r) -> p n r", r=2)
             for (uu, start, width, v_width, raw) in raws:
@@ -76,18 +76,21 @@ def tile_routed_moe_kernel(tc, xT, w_words, w_scales, b, gate, offs, out):
                 src = raw[:].rearrange("p r n -> p n r")
                 nc.vector.tensor_copy(pair[:, start : start + v_width, :], src[:, :v_width, :])
                 nc.scalar.copy(pair[:, start + v_width : start + width, :], src[:, v_width:, :])
-            for g in range(SLOTS // GATHER):
-                idx = offsets[:, g * GATHER // IDX_COL : (g + 1) * GATHER // IDX_COL]
-                dst = grouped[g][:].bitcast(U32).rearrange("p (n u) -> p n u", u=2)[:, :, u]
-                nc.vector.tensor_copy(dst, pairs[u][:].bitcast(U32).indirect(idx))
+            start = 0
+            for n in GATHERS[u]:
+                idx = offsets[:, start // IDX_COL : (start + n) // IDX_COL]
+                nc.vector.tensor_copy(gathered[:, u, start : start + n], pairs[u][:].bitcast(U32).indirect(idx))
+                start += n
 
         for s in range(SLOTS // SLICE):
             codes = held.tile([P, SLICE], U32, name=f"codes_{s}", align_bytes=64)
             scales = held.tile([P, SLICE], U8, name=f"scales_{s}", align_bytes=64)
-            g, off = divmod(s * SLICE, GATHER)
-            nc.vector.quantize_mx(
-                out=codes[:].bitcast(FP8X4), scales=scales[:], in_=grouped[g][:, 4 * off : 4 * (off + SLICE)]
+            grouped = held.tile([P, 4 * SLICE], BF16, name=f"grouped_{s}", align_bytes=64)
+            nc.scalar.copy(
+                grouped[:].bitcast(U32).rearrange("p (n u) -> p n u", u=2),
+                gathered[:, :, s * SLICE : (s + 1) * SLICE].rearrange("p u n -> p n u"),
             )
+            nc.vector.quantize_mx(out=codes[:].bitcast(FP8X4), scales=scales[:], in_=grouped[:])
             acc = psum.tile([P, SLICE], F32, name=f"acc_{s}")
             sums = held.tile([P, SLICE], F32, name=f"sums_{s}")
             for i in range(SLICE // C):

@@ -18,10 +18,9 @@ FLOPS = 2 * K * N * SLOTS
 IDX_COL = 16
 SLICE = 512
 PIECES = (
-    ((1024, 512), (1024, 512), (1024, 512), (1024, 512)),
-    ((1024, 512), (1024, 512), (1024, 512), (512, 320), (512, 320)),
+    ((1024, 512), (1024, 512), (1024, 512), (1024, 704)),
+    ((1024, 256), (1024, 512), (1024, 512), (512, 256), (256, 0), (256, 256)),
 )
-GATHERS = ((1024, 1024), (512, 512, 512, 512))
 
 
 def tile_routed_moe_kernel(tc, xT, w_words, w_scales, b, gate, offs, out):
@@ -57,42 +56,45 @@ def tile_routed_moe_kernel(tc, xT, w_words, w_scales, b, gate, offs, out):
         w_codes = held.tile([P, E * N], U32, name="w_codes", align_bytes=64)
         words_view = w_words.rearrange("e a p n r -> p (e a) (n r)").bitcast(I32)
         w_codes_view = w_codes[:].rearrange("p (e n) -> p e n", e=E).bitcast(I32)
+        gate_sb = held.tile([P, SLOTS], F32, name="gate_sb")
         for h in range(2):
             es = slice(h * E // 2, (h + 1) * E // 2)
             nc.sync.dma_start(w_codes_view[:, es, :], words_view[:, es, :])
-        gates = []
-        for h in range(2):
-            g = held.tile([P, SLOTS // 2], F32, name=f"gate_{h}")
-            nc.sync.dma_start(g[:], gate[:, h * (SLOTS // 2) : (h + 1) * (SLOTS // 2)])
-            gates.append(g)
+            cols = slice(h * SLOTS // 2, (h + 1) * SLOTS // 2)
+            nc.sync.dma_start(gate_sb[:, cols], gate[:, cols])
 
         pairs = [held.tile([P, 2 * T], BF16, name=f"pair_{u}") for u in range(2)]
         gathered = held.tile([P, 2, SLOTS], U32, name="gathered")
-        for u in range(2):
+        sums = held.tile([P, SLOTS], F32, name="sums")
+
+        def round_pair(u):
             pair = pairs[u][:].rearrange("p (n r) -> p n r", r=2)
             for (uu, start, width, v_width, raw) in raws:
                 if uu != u:
                     continue
                 src = raw[:].rearrange("p r n -> p n r")
-                nc.vector.tensor_copy(pair[:, start : start + v_width, :], src[:, :v_width, :])
-                nc.scalar.copy(pair[:, start + v_width : start + width, :], src[:, v_width:, :])
-            start = 0
-            for n in GATHERS[u]:
-                idx = offsets[:, start // IDX_COL : (start + n) // IDX_COL]
-                nc.vector.tensor_copy(gathered[:, u, start : start + n], pairs[u][:].bitcast(U32).indirect(idx))
-                start += n
+                if v_width > 0:
+                    nc.vector.tensor_copy(pair[:, start : start + v_width, :], src[:, :v_width, :])
+                if v_width < width:
+                    nc.scalar.copy(pair[:, start + v_width : start + width, :], src[:, v_width:, :])
 
-        for s in range(SLOTS // SLICE):
-            codes = held.tile([P, SLICE], U32, name=f"codes_{s}", align_bytes=64)
-            scales = held.tile([P, SLICE], U8, name=f"scales_{s}", align_bytes=64)
+        def gather(u, start, n):
+            idx = offsets[:, start // IDX_COL : (start + n) // IDX_COL]
+            nc.vector.tensor_copy(gathered[:, u, start : start + n], pairs[u][:].bitcast(U32).indirect(idx))
+
+        def interleave(s):
             grouped = held.tile([P, 4 * SLICE], BF16, name=f"grouped_{s}", align_bytes=64)
             nc.scalar.copy(
                 grouped[:].bitcast(U32).rearrange("p (n u) -> p n u", u=2),
                 gathered[:, :, s * SLICE : (s + 1) * SLICE].rearrange("p u n -> p n u"),
             )
+            return grouped
+
+        def multiply(s, grouped):
+            codes = held.tile([P, SLICE], U32, name=f"codes_{s}", align_bytes=64)
+            scales = held.tile([P, SLICE], U8, name=f"scales_{s}", align_bytes=64)
             nc.vector.quantize_mx(out=codes[:].bitcast(FP8X4), scales=scales[:], in_=grouped[:])
             acc = psum.tile([P, SLICE], F32, name=f"acc_{s}")
-            sums = held.tile([P, SLICE], F32, name=f"sums_{s}")
             for i in range(SLICE // C):
                 e = s * (SLICE // C) + i
                 cols = slice(i * C, (i + 1) * C)
@@ -108,16 +110,27 @@ def tile_routed_moe_kernel(tc, xT, w_words, w_scales, b, gate, offs, out):
                 )
             for i in range(SLICE // C):
                 e = s * (SLICE // C) + i
-                cols = slice(i * C, (i + 1) * C)
                 nc.scalar.activation(
-                    sums[:, cols], acc[:, cols], mybir.ActivationFunctionType.Identity, bias=bias[:, e : e + 1]
+                    sums[:, e * C : (e + 1) * C],
+                    acc[:, i * C : (i + 1) * C],
+                    mybir.ActivationFunctionType.Identity,
+                    bias=bias[:, e : e + 1],
                 )
-            h, off = divmod(s * SLICE, SLOTS // 2)
-            nc.vector.tensor_tensor(
-                window[:].indirect(offsets[:, s * SLICE // IDX_COL : (s + 1) * SLICE // IDX_COL]),
-                sums[:],
-                gates[h][:, off : off + SLICE],
-                mybir.AluOpType.mult,
-            )
+
+        round_pair(0)
+        for start in range(0, SLOTS, 1024):
+            gather(0, start, 1024)
+        round_pair(1)
+        groups = {}
+        for step in range(6):
+            if step < 4:
+                gather(1, step * SLICE, SLICE)
+                groups[step] = interleave(step)
+            if step >= 2:
+                multiply(step - 2, groups[step - 2])
+        for start, n in ((0, 512), (512, 512), (1024, 1024)):
+            idx = offsets[:, start // IDX_COL : (start + n) // IDX_COL]
+            cols = slice(start, start + n)
+            nc.vector.tensor_tensor(window[:].indirect(idx), sums[:, cols], gate_sb[:, cols], mybir.AluOpType.mult)
         nc.sync.dma_start(out[:, : T // 2], window[:, : T // 2])
         nc.scalar.dma_start(out[:, T // 2 :], window[:, T // 2 :])

@@ -19,7 +19,7 @@ IDX_COL = 16
 SLICE = 512
 PIECES = (
     ((1024, 512), (1024, 512), (1024, 512), (1024, 704)),
-    ((1024, 256), (1024, 512), (1024, 512), (512, 256), (256, 0), (256, 256)),
+    ((1024, 256), (1024, 512), (1024, 512), (640, 320), (384, 384)),
 )
 
 
@@ -48,18 +48,19 @@ def tile_routed_moe_kernel(tc, xT, w_words, w_scales, b, gate, offs, out):
         window = held.tile([P, T], F32, name="window")
         nc.vector.memset(window[:], 0.0)
 
-        sc_view = w_scales.rearrange("e a q n -> q (e a) n").bitcast(I32)
-        w_sc_view = w_sc[:].rearrange("p (e n) -> p e n", e=E).bitcast(I32)
-        for q in range(4):
-            nc.sync.dma_start(w_sc_view[32 * q : 32 * q + 4], sc_view[4 * q : 4 * q + 4])
-        nc.sync.dma_start(bias[:], b)
         w_codes = held.tile([P, E * N], U32, name="w_codes", align_bytes=64)
         words_view = w_words.rearrange("e a p n r -> p (e a) (n r)").bitcast(I32)
         w_codes_view = w_codes[:].rearrange("p (e n) -> p e n", e=E).bitcast(I32)
         gate_sb = held.tile([P, SLOTS], F32, name="gate_sb")
+        sc_view = w_scales.rearrange("e a q n -> q (e a) n").bitcast(I32)
+        w_sc_view = w_sc[:].rearrange("p (e n) -> p e n", e=E).bitcast(I32)
         for h in range(2):
             es = slice(h * E // 2, (h + 1) * E // 2)
             nc.sync.dma_start(w_codes_view[:, es, :], words_view[:, es, :])
+            if h == 0:
+                for q in range(4):
+                    nc.sync.dma_start(w_sc_view[32 * q : 32 * q + 4], sc_view[4 * q : 4 * q + 4])
+                nc.sync.dma_start(bias[:], b)
             cols = slice(h * SLOTS // 2, (h + 1) * SLOTS // 2)
             nc.sync.dma_start(gate_sb[:, cols], gate[:, cols])
 

@@ -15,11 +15,12 @@ K, T, E, C, N = 512, 4096, 16, 128, 128
 SLOTS = E * C
 FLOPS = 2 * K * N * SLOTS
 
+RUN = 4
 IDX_COL = 16
 SLICE = 512
 PIECES = (
-    ((1024, 512), (1024, 512), (1024, 512), (1024, 704)),
-    ((1024, 256), (1024, 512), (1024, 512), (640, 320), (384, 384)),
+    ((2048, 1152), (1024, 512), (1024, 704)),
+    ((2048, 512), (1024, 704), (768, 512), (256, 256)),
 )
 
 
@@ -73,11 +74,16 @@ def tile_routed_moe_kernel(tc, xT, w_words, w_scales, b, gate, offs, out):
             for (uu, start, width, v_width, raw) in raws:
                 if uu != u:
                     continue
-                src = raw[:].rearrange("p r n -> p n r")
-                if v_width > 0:
-                    nc.vector.tensor_copy(pair[:, start : start + v_width, :], src[:, :v_width, :])
+                dst = pair[:, start : start + width, :]
+                nc.vector.tensor_copy(
+                    dst[:, :v_width, :].rearrange("p (c i) r -> p c r i", i=RUN),
+                    raw[:, :, :v_width].rearrange("p r (c i) -> p c r i", i=RUN),
+                )
                 if v_width < width:
-                    nc.scalar.copy(pair[:, start + v_width : start + width, :], src[:, v_width:, :])
+                    nc.scalar.copy(
+                        dst[:, v_width:, :].rearrange("p (c i) r -> p c r i", i=RUN),
+                        raw[:, :, v_width:].rearrange("p r (c i) -> p c r i", i=RUN),
+                    )
 
         def gather(u, start, n):
             idx = offsets[:, start // IDX_COL : (start + n) // IDX_COL]
@@ -86,8 +92,8 @@ def tile_routed_moe_kernel(tc, xT, w_words, w_scales, b, gate, offs, out):
         def interleave(s):
             grouped = held.tile([P, 4 * SLICE], BF16, name=f"grouped_{s}", align_bytes=64)
             nc.scalar.copy(
-                grouped[:].bitcast(U32).rearrange("p (n u) -> p n u", u=2),
-                gathered[:, :, s * SLICE : (s + 1) * SLICE].rearrange("p u n -> p n u"),
+                grouped[:].bitcast(U32).rearrange("p (c i u) -> p c u i", i=RUN, u=2),
+                gathered[:, :, s * SLICE : (s + 1) * SLICE].rearrange("p u (c i) -> p c u i", i=RUN),
             )
             return grouped
 

from contextlib import ExitStack

import concourse.mybir as mybir

F32 = mybir.dt.float32
BF16 = mybir.dt.bfloat16
I32 = mybir.dt.int32
U32 = mybir.dt.uint32
U16 = mybir.dt.uint16
U8 = mybir.dt.uint8
FP8X4 = mybir.dt.float8_e4m3fn_x4

P = 128
K, T, E, C, N = 512, 4096, 16, 128, 128
SLOTS = E * C
FLOPS = 2 * K * N * SLOTS

RUN = 4
IDX_COL = 16
SLICE = 512
PIECES = (
    ((2048, 1152), (1024, 512), (1024, 704)),
    ((2048, 512), (1024, 704), (768, 512), (256, 256)),
)


def tile_routed_moe_kernel(tc, xT, w_words, w_scales, b, gate, offs, out):
    nc = tc.nc
    with ExitStack() as ctx:
        held = ctx.enter_context(tc.tile_pool(name="held", bufs=1))
        psum = ctx.enter_context(tc.psum_pool(name="psum", bufs=1))

        offsets = held.tile([P, SLOTS // IDX_COL], U16, name="offsets")
        x_view = xT.rearrange("(p u r) n -> u p r n", u=2, r=2)
        raws = []
        for u in range(2):
            start = 0
            for i, (width, v_width) in enumerate(PIECES[u]):
                raw = held.tile([P, 2, width], F32, name=f"raw_{u}_{i}")
                nc.sync.dma_start(raw[:], x_view[u][:, :, start : start + width])
                raws.append((u, start, width, v_width, raw))
                start += width
            if u == 0:
                nc.sync.dma_start(offsets[:], offs)

        bias = held.tile([P, E], F32, name="bias")
        w_sc = held.tile([P, E * N], U8, name="w_sc", align_bytes=64)
        nc.vector.memset(w_sc[:].bitcast(I32), 0)
        window = held.tile([P, T], F32, name="window")
        nc.vector.memset(window[:], 0.0)

        w_codes = held.tile([P, E * N], U32, name="w_codes", align_bytes=64)
        words_view = w_words.rearrange("e a p n r -> p (e a) (n r)").bitcast(I32)
        w_codes_view = w_codes[:].rearrange("p (e n) -> p e n", e=E).bitcast(I32)
        gate_sb = held.tile([P, SLOTS], F32, name="gate_sb")
        sc_view = w_scales.rearrange("e a q n -> q (e a) n").bitcast(I32)
        w_sc_view = w_sc[:].rearrange("p (e n) -> p e n", e=E).bitcast(I32)
        for h in range(2):
            es = slice(h * E // 2, (h + 1) * E // 2)
            nc.sync.dma_start(w_codes_view[:, es, :], words_view[:, es, :])
            if h == 0:
                for q in range(4):
                    nc.sync.dma_start(w_sc_view[32 * q : 32 * q + 4], sc_view[4 * q : 4 * q + 4])
                nc.sync.dma_start(bias[:], b)
            cols = slice(h * SLOTS // 2, (h + 1) * SLOTS // 2)
            nc.sync.dma_start(gate_sb[:, cols], gate[:, cols])

        pairs = [held.tile([P, 2 * T], BF16, name=f"pair_{u}") for u in range(2)]
        gathered = held.tile([P, 2, SLOTS], U32, name="gathered")
        sums = held.tile([P, SLOTS], F32, name="sums")

        def round_pair(u):
            pair = pairs[u][:].rearrange("p (n r) -> p n r", r=2)
            for (uu, start, width, v_width, raw) in raws:
                if uu != u:
                    continue
                dst = pair[:, start : start + width, :]
                nc.vector.tensor_copy(
                    dst[:, :v_width, :].rearrange("p (c i) r -> p c r i", i=RUN),
                    raw[:, :, :v_width].rearrange("p r (c i) -> p c r i", i=RUN),
                )
                if v_width < width:
                    nc.scalar.copy(
                        dst[:, v_width:, :].rearrange("p (c i) r -> p c r i", i=RUN),
                        raw[:, :, v_width:].rearrange("p r (c i) -> p c r i", i=RUN),
                    )

        def gather(u, start, n):
            idx = offsets[:, start // IDX_COL : (start + n) // IDX_COL]
            nc.vector.tensor_copy(gathered[:, u, start : start + n], pairs[u][:].bitcast(U32).indirect(idx))

        def interleave(s):
            grouped = held.tile([P, 4 * SLICE], BF16, name=f"grouped_{s}", align_bytes=64)
            nc.scalar.copy(
                grouped[:].bitcast(U32).rearrange("p (c i u) -> p c u i", i=RUN, u=2),
                gathered[:, :, s * SLICE : (s + 1) * SLICE].rearrange("p u (c i) -> p c u i", i=RUN),
            )
            return grouped

        def multiply(s, grouped):
            codes = held.tile([P, SLICE], U32, name=f"codes_{s}", align_bytes=64)
            scales = held.tile([P, SLICE], U8, name=f"scales_{s}", align_bytes=64)
            nc.vector.quantize_mx(out=codes[:].bitcast(FP8X4), scales=scales[:], in_=grouped[:])
            acc = psum.tile([P, SLICE], F32, name=f"acc_{s}")
            for i in range(SLICE // C):
                e = s * (SLICE // C) + i
                cols = slice(i * C, (i + 1) * C)
                w_cols = slice(e * N, (e + 1) * N)
                nc.tensor.matmul_mx(
                    out=acc[:, cols],
                    lhsT=w_codes[:, w_cols].bitcast(FP8X4),
                    lhsT_scale=w_sc[:, w_cols],
                    rhs=codes[:, cols].bitcast(FP8X4),
                    rhs_scale=scales[:, cols],
                    start=True,
                    stop=True,
                )
            for i in range(SLICE // C):
                e = s * (SLICE // C) + i
                nc.scalar.activation(
                    sums[:, e * C : (e + 1) * C],
                    acc[:, i * C : (i + 1) * C],
                    mybir.ActivationFunctionType.Identity,
                    bias=bias[:, e : e + 1],
                )

        round_pair(0)
        for start in range(0, SLOTS, 1024):
            gather(0, start, 1024)
        round_pair(1)
        groups = {}
        for step in range(6):
            if step < 4:
                gather(1, step * SLICE, SLICE)
                groups[step] = interleave(step)
            if step >= 2:
                multiply(step - 2, groups[step - 2])
        for start, n in ((0, 512), (512, 512), (1024, 1024)):
            idx = offsets[:, start // IDX_COL : (start + n) // IDX_COL]
            cols = slice(start, start + n)
            nc.vector.tensor_tensor(window[:].indirect(idx), sums[:, cols], gate_sb[:, cols], mybir.AluOpType.mult)
        nc.sync.dma_start(out[:, : T // 2], window[:, : T // 2])
        nc.scalar.dma_start(out[:, T // 2 :], window[:, T // 2 :])
